import numpy as np
import ml_dtypes


def mxq(x, axis, fmt="e4m3"):
    dtype, down = {"e4m3": (ml_dtypes.float8_e4m3fn, 7), "e5m2": (ml_dtypes.float8_e5m2, 14)}[fmt]
    v = np.moveaxis(np.asarray(x, np.float32).astype(ml_dtypes.bfloat16).astype(np.float64), axis, -1)
    blocks = v.reshape(v.shape[:-1] + (-1, 32))
    amax = np.abs(blocks).max(-1, keepdims=True)
    byte = np.maximum(np.where(amax > 0, np.frexp(amax)[1] - 1 + 127, 0) - down, 1)
    scale = np.exp2(byte - 127.0)
    codes = (blocks / scale).astype(np.float32).astype(dtype).astype(np.float64)
    return np.moveaxis((codes * scale).reshape(v.shape), -1, axis)


WIDE = False


def mx_kscale(k):
    if not WIDE:
        return np.ones(k)
    levels = np.array([10, -10, 5, -5, 0])
    if k % 512:
        return np.exp2(np.random.permutation(np.resize(levels, k // 32))).repeat(32)
    a = np.empty((k // 512, 16))
    for p in range(k // 512):
        a[p, :8] = np.random.permutation(np.resize(levels, 8))
        for g in range(8):
            far = levels[np.abs(levels - a[p, g]) >= 10]
            a[p, g + 8] = far[np.random.randint(len(far))]
    return np.exp2(a.ravel()).repeat(32)


def f64(x):
    return np.asarray(x).astype(np.float64)


def striped8(idx):
    return np.asarray(idx).reshape(8, -1, 16).transpose(0, 2, 1).reshape(128, -1).astype(np.uint16)


def unstriped8(offs):
    return offs.reshape(8, 16, -1).transpose(0, 2, 1).reshape(8, -1).astype(np.int64)


def pick8(x, idx, run):
    r = np.arange(len(x))
    return x[r[:, None], idx[r % (8 * run) // run]]


E2M1 = np.array([0.0, 0.5, 1.0, 1.5, 2.0, 3.0, 4.0, 6.0, -0.0, -0.5, -1.0, -1.5, -2.0, -3.0, -4.0, -6.0])


def pack_weight(w, fmt):
    k, n = w.shape
    w = f64(np.asarray(w, np.float32).astype(ml_dtypes.bfloat16)).reshape(k // 32, 32, n)
    amax = np.abs(w).max(1)
    if fmt == "e4m3":
        byte = np.frexp(amax)[1] - 1 + 127 - 7
    else:
        mant, ex = np.frexp(amax / 6.0)
        byte = np.where(mant > 0.5, ex, ex - 1) + 127
    byte = np.clip(np.where(amax > 0, byte, 1), 1, 254)
    scaled = (w * np.exp2(127.0 - byte)[:, None, :]).reshape(k, n).astype(np.float32)
    by_word = np.ascontiguousarray(scaled.reshape(k // 512, 128, 4, n).transpose(0, 1, 3, 2))
    if fmt == "e4m3":
        words = by_word.astype(ml_dtypes.float8_e4m3fn).view(np.uint8)
    else:
        c = by_word.astype(ml_dtypes.float4_e2m1fn).view(np.uint8) & 0xF
        words = (c[..., 0::2] | (c[..., 1::2] << 4)).reshape(k // 512, 128, 2 * n)
    return np.ascontiguousarray(words), np.ascontiguousarray(byte.astype(np.uint8).reshape(k // 512, 16, n))


def unpack_weight(words, scales, fmt):
    g, _, n = scales.shape
    words = np.ascontiguousarray(words).reshape(g, 128, n, -1)
    if fmt == "e4m3":
        vals = words.view(ml_dtypes.float8_e4m3fn).astype(np.float64)
    else:
        nib = np.empty((g, 128, n, 4), np.uint8)
        nib[..., 0::2] = words & 0xF
        nib[..., 1::2] = words >> 4
        vals = E2M1[nib]
    vals = vals * np.repeat(np.exp2(scales.astype(np.float64) - 127.0), 8, axis=1)[..., None]
    return vals.transpose(0, 1, 3, 2).reshape(g * 512, n)


D, T, I, Q = 512, 1024, 512, 128


def setup_inputs():
    n = np.random.standard_normal
    idx = np.stack([np.random.permutation(T)[:I] for _ in range(8)])
    idx2 = np.stack([np.random.permutation(T)[:I] for _ in range(8)])
    idx3 = np.stack([np.random.permutation(T)[:I] for _ in range(8)])
    fd = mx_kscale(D)
    keysp = pack_weight(n((D, T)) / fd[:, None], "e2m1")
    return {
        "query": (n((D, Q)) * 1.0 / np.sqrt(D) * fd[:, None]).astype(np.float32),
        "keys_words": keysp[0],
        "keys_scales": keysp[1],
        "old": (1.0 * n((Q, T))).astype(np.float32),
        "offs": striped8(idx),
        "offs2": striped8(idx2),
        "offs3": striped8(idx3),
    }


def reference(query, keys_words, keys_scales, old, offs, offs2, offs3):
    idx = unstriped8(offs)
    idx2 = unstriped8(offs2)
    idx3 = unstriped8(offs3)
    keysu = unpack_weight(keys_words, keys_scales, "e2m1")
    queryq = mxq(f64(query), 0, "e4m3")
    a = queryq.T @ keysu
    s = pick8(a, idx, 16) - pick8(a, idx2, 16)
    p = np.exp(s - np.max(s, axis=1, keepdims=True))
    w = p / np.sum(p, axis=1, keepdims=True)
    ws = w * 256.0
    f1 = np.zeros((Q, T))
    f1[np.arange(Q)[:, None], idx[np.arange(Q) % 128 // 16]] = ws
    f2 = f1 + f64(old)
    y = pick8(f2, idx3, 16)
    return y

from contextlib import ExitStack

import concourse.mybir as mybir

D, T, I, Q = 512, 1024, 512, 128
FLOPS = 2 * D * T * Q

F32 = mybir.dt.float32
BF16 = mybir.dt.bfloat16
I32 = mybir.dt.int32
U32 = mybir.dt.uint32
U16 = mybir.dt.uint16
U8 = mybir.dt.uint8
FP8X4 = mybir.dt.float8_e4m3fn_x4
FP4X4 = mybir.dt.float4_e2m1fn_x4
ALU = mybir.AluOpType
ACT = mybir.ActivationFunctionType
AXIS_X = mybir.AxisListType.X

P = 128
PACK = 4
HALF = I // 2
SCORE_WIDTHS = (256, 256, 256, 128, 128)


def tile_attend_difference_soft_through_heads_kernel(tc, query, keys_words, keys_scales, old, offs, offs2, offs3, out):
    nc = tc.nc
    with ExitStack() as ctx:
        sb = ctx.enter_context(tc.tile_pool(name="sb", bufs=1))
        ps = ctx.enter_context(tc.psum_pool(name="ps", bufs=1))

        list1 = sb.tile([P, I // 16], U16, name="list1")
        list2 = sb.tile([P, I // 16], U16, name="list2")
        list3 = sb.tile([P, I // 16], U16, name="list3")
        q_raw = sb.tile([P, PACK, Q], F32, name="q_raw", align_bytes=64)
        q_bf = sb.tile([P, Q, PACK], BF16, name="q_bf", align_bytes=64)
        q_codes = sb.tile([P, Q], U32, name="q_codes", align_bytes=64)
        q_scales = sb.tile([P, Q], U8, name="q_scales", align_bytes=64)
        k_words = sb.tile([P, 2 * T], U8, name="k_words", align_bytes=64)
        k_scales = sb.tile([P, T], U8, name="k_scales", align_bytes=64)
        old_sb = sb.tile([P, T], F32, name="old_sb", align_bytes=64)
        a = sb.tile([P, T], F32, name="a", align_bytes=64)
        x0 = sb.tile([P, HALF], F32, name="x0", align_bytes=64)
        x1 = sb.tile([P, HALF], F32, name="x1", align_bytes=64)
        y1 = sb.tile([P, HALF], F32, name="y1", align_bytes=64)
        neg_s = sb.tile([P, I], F32, name="neg_s", align_bytes=64)
        neg_max = sb.tile([P, 1], F32, name="neg_max")
        p = sb.tile([P, I], F32, name="p", align_bytes=64)
        total = sb.tile([P, 1], F32, name="total")
        inv_total = sb.tile([P, 1], F32, name="inv_total")
        ws = sb.tile([P, I], F32, name="ws", align_bytes=64)
        f1 = sb.tile([P, T], F32, name="f1", align_bytes=64)
        f2 = sb.tile([P, T], F32, name="f2", align_bytes=64)
        y_lo = sb.tile([P, HALF], F32, name="y_lo", align_bytes=64)
        y_hi = sb.tile([P, HALF], F32, name="y_hi", align_bytes=64)

        nc.vector.memset(k_scales[:].bitcast(I32), 0)
        nc.vector.memset(f1[:], 0.0)

        nc.sync.dma_start(out=q_raw[:], in_=query.rearrange("(p j) q -> p j q", j=PACK))
        nc.sync.dma_start(out=k_words[:].bitcast(I32), in_=keys_words[0].bitcast(I32))
        for quad in range(4):
            nc.scalar.dma_start(
                out=k_scales[32 * quad : 32 * quad + 4, :].bitcast(I32),
                in_=keys_scales[0, 4 * quad : 4 * quad + 4, :].bitcast(I32),
            )
        nc.sync.dma_start(list1[:], offs)
        nc.sync.dma_start(list2[:], offs2)
        nc.sync.dma_start(out=old_sb[:], in_=old)
        nc.sync.dma_start(list3[:], offs3)

        nc.vector.tensor_copy(
            out=q_bf[:].rearrange("p (c i) t -> p c t i", i=4),
            in_=q_raw[:].rearrange("p t (c i) -> p c t i", i=4),
        )
        nc.vector.quantize_mx(
            out=q_codes[:].bitcast(FP8X4), scales=q_scales[:], in_=q_bf[:].rearrange("p q t -> p (q t)")
        )

        t0 = 0
        for b, width in enumerate(SCORE_WIDTHS):
            bank = ps.tile([P, width], F32, name=f"bank{b}")
            nc.tensor.matmul_mx(
                out=bank[:],
                lhsT=q_codes[:].bitcast(FP8X4),
                lhsT_scale=q_scales[:],
                rhs=k_words[:, 2 * t0 : 2 * (t0 + width)].bitcast(FP4X4),
                rhs_scale=k_scales[:, t0 : t0 + width],
                start=True,
                stop=True,
            )
            if b % 2 == 0:
                nc.vector.tensor_copy(out=a[:, t0 : t0 + width], in_=bank[:])
            else:
                nc.scalar.activation(out=a[:, t0 : t0 + width], in_=bank[:], func=ACT.Copy)
            t0 = t0 + width

        lo, hi = slice(0, HALF // 16), slice(HALF // 16, I // 16)
        nc.scalar.activation(out=x0[:], in_=a[:].indirect(list1[:, lo]), func=ACT.Copy)
        nc.vector.tensor_copy(out=y1[:], in_=a[:].indirect(list2[:, hi]))
        nc.scalar.activation(out=x1[:], in_=a[:].indirect(list1[:, hi]), func=ACT.Copy)
        nc.vector.tensor_tensor(neg_s[:, :HALF], a[:].indirect(list2[:, lo]), x0[:], ALU.subtract)
        nc.vector.tensor_tensor(neg_s[:, HALF:], y1[:], x1[:], ALU.subtract)
        nc.vector.tensor_reduce(out=neg_max[:], in_=neg_s[:], axis=AXIS_X, op=ALU.min)
        nc.scalar.activation(out=p[:], in_=neg_s[:], func=ACT.Exp, bias=neg_max[:], scale=-1.0, accum_out=total[:])
        nc.vector.reciprocal(out=inv_total[:], in_=total[:])
        nc.vector.tensor_scalar(ws[:], p[:], inv_total[:], 256.0, ALU.mult, ALU.mult)
        nc.vector.tensor_copy(out=f1[:].indirect(list1[:]), in_=ws[:])
        nc.vector.tensor_tensor(f2[:], f1[:], old_sb[:], ALU.add)
        nc.vector.tensor_copy(out=y_lo[:], in_=f2[:].indirect(list3[:, lo]))
        nc.scalar.activation(out=y_hi[:], in_=f2[:].indirect(list3[:, hi]), func=ACT.Copy)
        nc.sync.dma_start(out=out[:, :HALF], in_=y_lo[:])
        nc.scalar.dma_start(out=out[:, HALF:], in_=y_hi[:])
